import numpy as np, ml_dtypes
CORES = [1,5,17,21,33,37,49,53]
N = 8
BF = ml_dtypes.bfloat16
S, F, L, RO, A, TH, BYG = 4096, 768, 256, 3, 704, 8, 1
def whole(x, hi):
    return np.minimum(x.astype(np.int64), hi)
def parts(rng):
    a = rng.choice(np.array([0.2, 0.3, 0.4, 0.5]), (N, 8, 1, 1)).astype(np.float32)
    t = whole(256 * rng.random((N, 8, 16, S), dtype=np.float32) ** a, 255)
    t = np.where(rng.random((N, 8, 1, S)) < 0.25, 255, t)
    return t, rng.integers(0, 255, (N, 8, 16, F)), rng.integers(0, S, (N, 8, 16, F)), rng.integers(0, S, (N, 8, 16, F))
def pack(t, z, eh, ef):
    return {"tab": t.reshape(N, 128, S).astype(np.float32).astype(BF), "zf": z.reshape(N, 128, F).astype(np.float32).astype(BF),
            "eh": np.ascontiguousarray(eh.reshape(N, 128, F)).astype(np.int32), "ef": np.ascontiguousarray(ef.reshape(N, 128, F)).astype(np.int32)}
def setup_inputs(rng):
    return pack(*parts(rng))
def setup_inputs_full(rng):
    t, z, eh, ef = parts(rng)
    for g in (0, 5):
        t[:, g] = 255; eh[:, g] = rng.integers(F, S, (N, 16, F)); ef[:, g] = rng.integers(F, S, (N, 16, F))
        eh[:, g, 0] = np.argsort(rng.random((N, F)), axis=1)
    f = np.arange(F); c = F - A; see = (f >= A - c) & (f < A)
    m = np.flatnonzero(see)
    for g in (2, 7):
        p = np.argsort(rng.random((N, S // 2)), axis=1)[:, :L]
        t[:, g] = 255; eh[:, g] = rng.integers(S // 2, S - 64, (N, 16, F)); ef[:, g] = rng.integers(S // 2, S - 64, (N, 16, F))
        z[:, g] = np.where(f < L, rng.integers(160, 255, (N, 16, F)), np.where(see, rng.integers(100, 160, (N, 16, F)), rng.integers(0, 100, (N, 16, F))))
        eh[:, g, 0] = np.where(see, eh[:, g, 0], p[:, f % L])
        for r in range(N):
            q = (r + 1 + (2 + BYG * g) % (N - 1)) % N
            a, b = m[1::4], m[3::4]
            ef[r, g, rng.integers(0, 16, len(a)), a] = p[q, L - c - 1]
            ef[r, g, rng.integers(0, 16, len(b)), b] = np.max(p[q])
    return pack(t, z, eh, ef)
def setup_inputs_ties(rng):
    t, z, eh, ef = parts(rng)
    pat = np.array([0, 0, 2, 3, 5, TH - 2, TH - 2, TH - 2, TH - 1, TH - 1, TH - 1, TH - 1, TH, TH, TH, 16])
    place = np.argsort(rng.random((N, 4, 16, S), dtype=np.float32), axis=2)
    t[:, :4] = np.where(place < pat[np.arange(S) % 16], 0, 255)
    for x in (eh, ef):
        top = rng.choice(np.array([8, 12, 12, 12, 15, 16]), (N, 4, 1, F))
        x[:, :4] = 16 * rng.integers(0, S // 16, (N, 4, 16, F)) + (rng.random((N, 4, 16, F)) * top).astype(np.int64)
    v = np.array([0, 1, 127, 128, 254, 255])
    t[:, 4:] = rng.choice(v, (N, 4, 16, S), p=[0.04, 0.04, 0.1, 0.12, 0.3, 0.4]); z[:, 4:] = rng.choice(v[:5], (N, 4, 16, F))
    return pack(t, z, eh, ef)
def setup_inputs_alike(rng):
    t, z, eh, ef = parts(rng); few = np.array([0, S - 1, S // 2, 3])
    eh[:, 0] = rng.choice(few, (N, 16, F)); eh[:, 1] = rng.integers(0, S, (N, 1, F))
    t[:, 2] = 255; eh[:, 2] = rng.integers(0, S, (N, 1, 1))
    eh[:, 3] = S - 1 - rng.integers(0, 12, (N, 16, F)); ef[:, 3] = S - 1 - rng.integers(0, 12, (N, 16, F))
    ef[:, 4] = rng.choice(few, (N, 16, F))
    for x in (z, eh, ef): x[:, 5, :, 1::2] = x[:, 5, :, 0::2]
    return pack(t, z, eh, ef)
def setup_inputs_hard(rng):
    t, z, eh, ef = parts(rng)
    t[:, 0] = 0; t[rng.integers(0, N), 1] = 0; t[:, 2] = 255
    z[:, 3] = 0; t[:, 3] = np.maximum(t[:, 3], 1)
    z[:, 4] = 254; t[:, 4] = np.where(rng.random((N, 16, S)) < 0.8, 255, t[:, 4])
    return pack(t, z, eh, ef)
def setup_inputs_spread(rng):
    u = np.float32(2) ** -rng.integers(-2, 6, (N, 8, 1, S)).astype(np.float32); v = np.float32(2) ** rng.integers(-2, 5, (N, 8, 1, F)).astype(np.float32)
    t = whole(256 * rng.random((N, 8, 16, S), dtype=np.float32) ** u, 255); z = whole(255 * rng.random((N, 8, 16, F), dtype=np.float32) ** v, 254)
    e = [whole(S * rng.random((N, 8, 16, F)) ** (2.0 ** rng.integers(0, 3, (N, 8, 16, 1))), S - 1) for i in range(2)]
    return pack(t, z, e[0], e[1])
def check_inputs(d):
    bad = []
    for k, hi in (("tab", 255), ("zf", 254), ("eh", S - 1), ("ef", S - 1)):
        v = np.asarray(d[k]).astype(np.float64)
        if not (np.min(v) >= 0 and np.max(v) <= hi): bad.append("range of " + k)
        if not np.all(v == np.floor(v)): bad.append("whole numbers in " + k)
    return bad
def reference(tab, zf, eh, ef):
    t = tab.astype(np.float32).astype(np.int32).reshape(N, 8, 16, S); z = zf.astype(np.float32).astype(np.int32).reshape(N, 8, 16, F)
    home = eh.astype(np.int64).reshape(N, 8, 16, F); far = ef.astype(np.int64).reshape(N, 8, 16, F)
    d = np.zeros((N, 8, F), np.int64); oc = np.full((N, 8, S), -1, np.int64); free = np.ones((N, 8, F), bool)
    for step in range(RO):
        old = np.array(t)
        turn = (np.arange(F) + A * step) % F
        for r in range(N):
            for g in range(8):
                q = (r + 1 + (step + BYG * g) % (N - 1)) % N
                ln = turn[free[r, g][turn]][:L]
                zl = z[r, g][:, ln]
                sh = (home[r, g][:, ln] + d[r, g, ln]) & (S - 1); sf = (far[r, g][:, ln] + d[r, g, ln]) & (S - 1)
                ph = np.sum(old[r, g][:, sh] <= zl[:, None, :], axis=0); pf = np.sum(old[q, g][:, sf] <= zl[:, None, :], axis=0)
                k = np.argmax(ph, axis=0)
                worst = np.maximum(np.max(ph, axis=0), np.max(pf, axis=0)); go = worst < TH
                d[r, g, ln] += np.where(go, 0, worst)
                cl = np.flatnonzero(go)
                s, first = np.unique(sh[k, np.arange(L)][cl], return_index=True)
                w = cl[first]; was = oc[r, g, s]; was = was[was >= 0]
                d[r, g, was] += 1; free[r, g, was] = True
                t[r, g][:, s] = zl[:, w]; oc[r, g, s] = ln[w]; free[r, g, ln[w]] = False
    return {"yt": t.reshape(N, 128, S).astype(np.float32).astype(BF), "yo": oc.astype(np.float32), "yd": d.astype(np.float32)}

import numpy as np
from concourse.bass import DstId, RemoteDMATransfer
from concourse.mybir import AluOpType as A, AxisListType, ActivationFunctionType as AF

N, NG, NS, NF, NL = 8, 8, 4096, 768, 256
WR = 32
NT = NS + WR + 3 * NL
DUMP = NS + WR
TYPES = {"b": "bfloat16", "f": "float32", "i": "int32", "u": "uint16"}
SCRATCH = {"psb": ("psum", [128, 4096], "float32")}
for _where, _shape, _names in (
        ("sbuf", [128, NT], "b:tb b:f1 b:f2 f:occ"), ("sbuf", [128, NF], "i:eh_s i:ef_s b:z_s b:zf1 b:zf2 b:st f:stc b:ydm f:idf b:ihi b:ilo b:ihl"),
        ("sbuf", [128, 4096], "b:zrep b:zrepf b:cmph b:cmpf"), ("sbuf", [128, 2048], "b:nrow"),
        ("sbuf", [128, NL], "i:efq b:zql f:xp f:xf f:dc u:offh u:offf b:zl b:dl f:lnf1 f:lnf2 b:st1 f:st1c f:st2 b:b1 b:b3 b:zu "
                            "b:ctx b:gr b:gle b:glo b:ngt b:t1 b:junk i:rep_i u:rep"),
        ("sbuf", [128, 16], "u:w0 u:u10 u:u20 f:mk b:li"), ("sbuf", [128, 32], "u:w1 u:w2 u:u21"),
        ("sbuf", [128, N * 16], "u:la0"), ("sbuf", [128, N * 32], "u:la1"),
        ("sbuf", [128, 2, 64], "f:kh f:k1 b:fh b:m1"), ("sbuf", [128, 2, 32], "f:k2 b:m2"), ("sbuf", [128, 2, 16], "f:k3 b:m3"),
        ("sbuf", [128, 2, 8], "i:hki i:whi b:m4 b:wm b:ng b:go_ f:rr b:nd"), ("sbuf", [128, 8, 2], "b:wq b:wland"),
        ("sbuf", [128, 2, 24], "i:di b:sd b:sdg b:dd0 b:dd1 b:dd2"), ("sbuf", [128, 2, 40], "b:ttl"), ("sbuf", [128, 2, 56], "b:cdl"),
        ("sbuf", [128, 48], "b:uu f:vb b:scn f:dst u:dsu f:yc"),
        ("sbuf", [128, 8], "i:pc i:pmi f:ck f:pmf f:pcf b:blkf b:blkk"), ("sbuf", [128, 64], "i:li_i"), ("sbuf", [128, 144], "b:ew b:ela b:elb b:el"),
        ("sbuf", [128, 128], "f:pmx f:z32 b:idb b:err b:ere b:ero b:er b:er2 b:onb b:ntr"), ("sbuf", [128, 512], "b:ob"),
        ("sbuf", [128, 1024], "b:zb b:mmk b:ngc"),
        ("dram", [1024, 32], "i:rd b:zq i:rl b:zqd"), ("dram", [1024, 512], "b:td b:fd1 b:fd2"), ("dram", [1024, 96], "b:zd b:zd1 b:zd2"),
        ("dram", [128, NS], "b:hb"), ("dram", [128, NF], "b:hz")):
    for _n in _names.split():
        SCRATCH[_n[2:]] = (_where, _shape, TYPES[_n[0]])
ENG = {"v": "ev", "s": "es", "p": "ep", "g": "eg"}
SEMAPHORES = (["ev", "es", "ep", "eg", "lsem", "l_hb", "a_req", "a_wf", "a_l0", "a_l1", "a_f1", "a_f2", "a_hb", "a_hz"]
              + ["d%d" % k for k in range(24)])
WRITES = ("out", "accum_out", "ap")
MASKS = {}
ALL = slice(None)


def asked(r, g, t):
    return (r + 1 + (t + g) % (N - 1)) % N


def asker(q, g, t):
    return (q - 1 - (t + g) % (N - 1)) % N


def dst_id(topo, c):
    a = topo.addr(c)
    return DstId(rid=a[0], pnc=a[1])


def off_chip(topo, src, dst):
    return topo.chip(src) != topo.chip(dst)


def far_engines(core, T, topo):
    for c in T.cores:
        if off_chip(topo, core, c):
            return topo.engines(core, c)
    return []


def near_engines(core, dst, T, topo):
    far = far_engines(core, T, topo)
    return [e for e in topo.engines(core, dst) if e not in far]


def helper_of(core, T, topo):
    for c in topo.cores_of(core):
        if T.rank_of(c) is None and topo.die(c) == topo.die(core) and all(topo.may_write(c, d) for d in T.cores):
            return c


def singles(core, dsts, T, topo):
    nf, nn, out = 0, 0, []
    for d in dsts:
        if off_chip(topo, core, d):
            out.append(topo.engines(core, d)[nf])
            nf += 1
        else:
            out.append(near_engines(core, d, T, topo)[nn])
            nn += 1
    return out


def bits(engines):
    m = 0
    for e in engines:
        m |= 1 << e
    return m


def v(name, *idx):
    return ("v", name, idx if idx else (ALL,))


def ind(win, off):
    return ("i", win, off)


def is_view(x):
    return isinstance(x, tuple) and len(x) == 3 and x[0] in ("v", "i")


def region(view):
    name, idx = view[1], view[2]
    shape = SCRATCH[name][1]
    key = (name, str(idx))
    if key not in MASKS:
        a, b, c = idx[0].indices(shape[0])
        n = int(np.prod(shape[1:]))
        sel = np.arange(n).reshape(shape[1:])[tuple(idx[1:])] if len(idx) > 1 else np.arange(n)
        m = np.zeros(n, bool)
        m[np.asarray(sel).ravel()] = True
        bank = 0
        if SCRATCH[name][0] == "psum":
            for k in range(n // 512):
                if m[k * 512:(k + 1) * 512].any():
                    bank |= 1 << k
        MASKS[key] = (a, b, int.from_bytes(np.packbits(m).tobytes(), "big"), bank)
    return MASKS[key]


def flow(g, T):
    queues = {"v": g.vector, "s": g.scalar, "p": g.tensor, "g": g, "y": g.sync}
    known = {q: {} for q in queues}
    total, acc = {}, {}

    def ap(x):
        if x[0] == "i":
            return ap(x[1]).indirect(ap(x[2]))
        t = T[x[1]]
        return t[x[2] if len(x[2]) > 1 else x[2][0]]

    def parts(x):
        return [x] if x[0] == "v" else [x[1], x[2]]

    def each(reads, writes):
        for kind, xs in (("r", reads), ("w", writes)):
            for x in xs:
                if x[1] in SCRATCH:
                    yield kind, x[1], region(x)

    def deps(q, reads, writes, tile=None):
        ev = []
        for kind, name, (p0, p1, m, bank) in each(reads, writes):
            for e in acc.get(name, ()):
                if bank and (bank & e["bank"]) and (q != e["q"] or (tile is not None and e["tile"] not in (None, tile))):
                    ev.append(e["ev"])
                elif (kind == "w" or e["kind"] == "w") and e["p0"] < p1 and p0 < e["p1"] and (m & e["m"]):
                    if bank and q == "p" and e["q"] == "p":
                        continue
                    if kind == "w" and e["kind"] == "r" and q == e["q"] and q in ENG:
                        continue
                    ev.append(e["ev"])
        return ev

    def settle(q, ev):
        need = {}
        for sem, cnt, clk in ev:
            if sem not in need or need[sem][0] < cnt:
                need[sem] = (cnt, clk)
        for sem in sorted(need, key=lambda s: -sum(need[s][1].values())):
            cnt, clk = need[sem]
            if known[q].get(sem, 0) >= cnt:
                continue
            queues[q].wait_ge(T.sem[sem], cnt)
            for k in clk:
                known[q][k] = max(known[q].get(k, 0), clk[k])
            known[q][sem] = max(known[q].get(sem, 0), cnt)

    def note(q, reads, writes, event, tile=None):
        for kind, name, (p0, p1, m, bank) in each(reads, writes):
            old = acc.get(name, [])
            inside = lambda e: p0 <= e["p0"] and e["p1"] <= p1 and (e["m"] & ~m) == 0
            if kind == "w" and not bank:
                old = [e for e in old if not inside(e)]
            else:
                old = [e for e in old if not (e["kind"] == kind and e["q"] == q and e["ev"][0] == event[0] and inside(e))]
            acc[name] = old + [{"kind": kind, "q": q, "p0": p0, "p1": p1, "m": m, "bank": bank, "ev": event, "tile": tile}]

    def done(who, q, sem, n, reads, writes, tile=None):
        total[sem] = total.get(sem, 0) + n
        clk = dict(known[q])
        clk[sem] = total[sem]
        note(who, reads, writes, (sem, total[sem], clk), tile)

    def call(q, meth, **kw):
        reads, writes, tile = [], [], None
        for k in kw:
            x = kw[k]
            if is_view(x):
                if k in WRITES:
                    writes.append(parts(x)[0])
                    reads += parts(x)[1:]
                else:
                    reads += parts(x)
        if meth == "matmul":
            p0, p1, m, bank = region(kw["lhsT"])
            tile = p0 if p1 - p0 <= 32 else None
        settle(q, deps(q, reads, writes, tile))
        args = {k: (ap(kw[k]) if is_view(kw[k]) else kw[k]) for k in kw}
        eng = queues[q]
        f = {"tensor_copy": lambda: eng.tensor_copy(**args), "tensor_tensor": lambda: eng.tensor_tensor(**args),
             "tensor_scalar": lambda: eng.tensor_scalar(**args), "tensor_reduce": lambda: eng.tensor_reduce(**args),
             "scan": lambda: eng.tensor_tensor_scan(**args), "memset": lambda: eng.memset(args["ap"], args["constant"]),
             "activation": lambda: eng.activation(**args), "matmul": lambda: eng.matmul(**args),
             "iota": lambda: eng.iota(**args), "affine_select": lambda: eng.affine_select(**args)}[meth]
        f().then_inc(T.sem[ENG[q]], 1)
        done(q, q, ENG[q], 1, reads, writes, tile)

    def dma(q, sem, out, in_):
        settle(q, deps(q, [in_], [out]))
        queues[q].dma_start(out=ap(out), in_=ap(in_)).then_inc(T.sem[sem], 16)
        done(sem, q, sem, 16, [in_], [out])

    def arrive(out, sem, cnt):
        total[sem] = cnt
        note("far", [], [out], (sem, cnt, {sem: cnt}))

    def fused(transfers, local="lsem"):
        srcs = [t[0] for t in transfers]
        settle("g", deps("g", srcs, []))
        g.remote_dma_fused([RemoteDMATransfer(dst_ids=[d[0] for d in t[1]], dma_engine_mask=bits(t[2]), remote_sem=T.sem[t[3]],
                                              srcs=[ap(t[0])], dsts=[ap(d[1]) for d in t[1]]) for t in transfers],
                           local_sem=T.sem[local])
        done(local, "g", local, sum(len(t[2]) for t in transfers), srcs if local != "lsem" else [], [])

    def after(q, names):
        settle(q, [e["ev"] for n in names for e in acc.get(n, ())])

    def finish():
        for sem in total:
            if known["g"].get(sem, 0) < total[sem]:
                g.wait_ge(T.sem[sem], total[sem])

    return {"call": call, "dma": dma, "arrive": arrive, "fused": fused, "after": after, "finish": finish}


def blk(name, k):
    return v(name, slice(128 * k, 128 * k + 128), ALL)


def cols(name, a, b, step=None):
    return v(name, ALL, slice(a, b, step))


def rows(name, n, a, b, step=None):
    return v(name, slice(0, n), slice(a, b, step))


def sub(name, a, b):
    return v(name, ALL, ALL, slice(a, b))


def halves(a, n):
    return sub(a, 0, n), sub(a, n, 2 * n)


def helper_main(g, core, rank, T, topo):
    F = flow(g, T)
    F["arrive"](v("hb"), "a_hb", len(topo.engines(T.cores[rank], core)))
    F["arrive"](v("hz"), "a_hz", len(topo.engines(T.cores[rank], core)))
    F["dma"]("s", "d1", v("zd"), v("hz"))
    F["dma"]("y", "d0", v("td"), v("hb"))
    for t in (1, 2):
        dst = [T.cores[asker(rank, k, t)] for k in range(NG)]
        eng = singles(core, dst, T, topo)
        for src, land in (("zd", "zd%d" % t), ("td", "fd%d" % t)):
            F["fused"]([(blk(src, k), [(dst_id(topo, dst[k]), blk(land, k))], [eng[k]], "a_f%d" % t) for k in range(NG)])
    F["finish"]()


def rank_main(g, core, rank, T, topo):
    F = flow(g, T)
    C, dma, arrive, fused = F["call"], F["dma"], F["arrive"], F["fused"]
    ps = lambda a, b, n=128: v("psb", slice(0, n), slice(a, b))
    P6, P7 = 3072, 3584
    row = ps(P7 + 256, P7 + 512)

    def copy(q, out, in_):
        if q == "s":
            C("s", "activation", out=out, in_=in_, func=AF.Copy)
        else:
            C("v", "tensor_copy", out=out, in_=in_)

    def tt(out, a, b, op):
        C("v", "tensor_tensor", out=out, in0=a, in1=b, op=op)

    def ts(out, a, s1, op, s2=None, op1=None):
        if op1 is None:
            C("v", "tensor_scalar", out=out, in0=a, scalar1=s1, scalar2=None, op0=op)
        else:
            C("v", "tensor_scalar", out=out, in0=a, scalar1=s1, scalar2=s2, op0=op, op1=op1)

    def mm(out, lhsT, rhs, start=True, stop=True):
        C("p", "matmul", out=out, lhsT=lhsT, rhs=rhs, start=start, stop=stop)

    def fill(x, c):
        C("v", "memset", ap=x, constant=c)

    def iota(out, pattern, base, ch):
        if SCRATCH[out[1]][2] == "int32":
            C("g", "iota", out=out, pattern=pattern, base=base, channel_multiplier=ch)
        else:
            C("g", "iota", out=out, pattern=pattern, base=base, channel_multiplier=ch, allow_small_or_imprecise_dtypes=True)

    def sel(out, in_, pattern, op, fillv, base, ch):
        C("g", "affine_select", out=out, in_=in_, pattern=pattern, compare_op=op, fill=float(fillv), base=base, channel_multiplier=ch)

    dma("y", "d0", v("rd"), v("ef", ALL, slice(0, NL)))
    dma("s", "d1", v("zq"), v("zf", ALL, slice(0, NL)))
    dma("s", "d3", cols("z_s", 64, 320), v("zf", ALL, slice(0, NL)))
    dma("y", "d2", cols("eh_s", 64, 320), v("eh", ALL, slice(0, NL)))
    dma("y", "d4", cols("tb", 0, NS), v("tab"))

    iota(v("rep_i"), [[1, NL]], 0, 0)
    copy("v", v("rep"), v("rep_i"))
    iota(v("pc"), [[0, 8]], 0, 1)
    fill(v("z32"), 0.0)
    fill(v("ob"), 1.0)
    fill(v("zb"), 0.0)
    ts(v("pmi"), v("pc"), 15, A.bitwise_and)
    ts(v("ck"), v("pmi"), -8192.0, A.mult, 122880.0, A.add)
    copy("v", v("pmf"), v("pmi"))
    sel(v("pmx"), v("z32"), [[1, 16], [16, 8]], A.not_equal, 1.0, 0, -1)
    sel(v("blkf"), cols("ob", 0, 8), [[-16, 8]], A.is_ge, 0.0, 0, 1)
    sel(v("blkf"), v("blkf"), [[16, 8]], A.is_ge, 0.0, 15, -1)
    ckc, pmc = cols("ck", 0, 1), cols("pmf", 0, 1)

    dst = [T.cores[asked(rank, k, 0)] for k in range(NG)]
    eng = singles(core, dst, T, topo)
    for src, land in (("zq", "zqd"), ("rd", "rl")):
        fused([(blk(src, k), [(dst_id(topo, dst[k]), blk(land, k))], [eng[k]], "a_req") for k in range(NG)])
    arrive(v("rl"), "a_req", 2 * NG)
    arrive(v("zqd"), "a_req", 2 * NG)

    iota(v("li_i"), [[16, 64]], 0, 0)
    sel(v("idb"), cols("zb", 0, 128), [[1, 128]], A.not_equal, 1.0, 0, -1)
    ts(cols("mk", 0, 8), v("pmf"), 0.0, A.is_equal)
    ts(cols("mk", 8, 16), v("pmf"), 1.0, A.is_equal)
    ts(v("blkk"), v("blkf"), 131072.0, A.mult)
    ts(v("xp"), cols("eh_s", 64, 320), ckc, A.add)
    copy("v", v("offh"), cols("eh_s", 64, 320))
    copy("v", v("pcf"), v("pc"))
    for t in range(3):
        n = "dd%d" % t
        fill(sub(n, 0, 8), 8.0 + t)
        for h in range(2):
            fill(v(n, ALL, h, slice(8, 16)), -6.0 + 8 * h)
            ts(v(n, ALL, h, slice(16, 24)), v("pcf"), -8.0, A.add)
    fill(sub("cdl", 48, 56), 1.0)
    fill(v("st"), 0.0)
    fill(v("uu"), 1.0)
    fill(v("vb"), 0.0)
    fill(v("ntr"), -1.0)
    for name in ("err", "ere", "ero", "er", "er2"):
        copy("v", v(name), cols("zb", 0, 128))
    copy("v", v("ew"), cols("zb", 0, 144))
    ts(v("li"), cols("li_i", 0, 16), pmc, A.add)
    ts(v("yc"), cols("li_i", 0, 48), pmc, A.add, 961.0, A.add)

    def zrep(out, win, lists):
        for j in range(4):
            copy("s", cols(out, 1024 * j, 1024 * j + 1024), ind(win, cols(lists, 64 * j, 64 * j + 64)))

    def look(j, out, table, width, off, rep_):
        tt(cols(out, 1024 * j, 1024 * j + 1024), ind(cols(table, 0, width), cols(off, 64 * j, 64 * j + 64)),
           cols(rep_, 1024 * j, 1024 * j + 1024), A.is_le)

    def cmpcol(name, h, k):
        return cols(name, 2048 * h + k, 2048 * h + 2048, 16)

    def key_mm(h):
        b = 512 * h
        mm(ps(b, b + 128), cols("xp", 128 * h, 128 * h + 128), v("pmx"), True, False)
        for k in range(16):
            mm(ps(b + 8 * k, b + 8 * k + 8), cmpcol("cmph", h, k), v("blkk"), False, k == 15)
        copy("s", v("kh", ALL, h, ALL), ps(b + 64, b + 128))

    def home_tree(t):
        for h in range(2):
            tt(v("k1", ALL, h, ALL), ps(512 * h, 512 * h + 64), v("kh", ALL, h, ALL), A.max)
        tt(v("k2"), *halves("k1", 32), A.max)
        tt(v("k3"), *halves("k2", 16), A.max)
        tt(v("hki"), *halves("k3", 8), A.max)
        for q, sh in ((0, 8), (1, 4)):
            ts(sub("di", 8 * q, 8 * q + 8), v("hki"), sh, A.arith_shift_right, 15, A.bitwise_and)
        ts(sub("di", 16, 24), v("hki"), 15, A.bitwise_and)
        ts(v("whi"), v("hki"), 17, A.arith_shift_right)
        ts(sub("cdl", 0, 24), v("di"), -8.0, A.add)
        C("s", "activation", out=sub("cdl", 24, 48), in_=sub("cdl", 0, 24), func=AF.Square)
        tt(v("sd"), sub("cdl", 0, 24), v("dd%d" % t), A.subtract)

    def gram_rows():
        for h in range(2):
            mm(ps(P7 + 128 * h, P7 + 128 * h + 128, 56), v("cdl", ALL, h, ALL), v("idb"))
        ct = rows("ctx", 56, 0, NL)
        copy("s", ct, ps(P7, P7 + NL, 56))
        for name, e, b in (("gr", "err", P7 + 256), ("gle", "ere", 0), ("glo", "ero", 256)):
            mm(ps(b, b + NL), rows(e, 56, 0, 128), ct)
        for name, b in (("gr", P7 + 256), ("gle", 0), ("glo", 256)):
            copy("s", v(name), ps(b, b + NL))

    def masks(bs):
        for b in bs:
            mm(ps(512 * b, 512 * b + 512), v("idb"), cols("mmk", 0, 512) if b < 4 else cols("mmk", 512, 1024), True, False)

    def blocks():
        out = []
        for b in (3, 2, 5, 4, 1, 0):
            if b < 4:
                out += [(2 * b + x, 1, 512 * b + 256 * x, 256) for x in range(2)]
            else:
                out += [(4 * (b - 4) + x, 0, 512 * b + 128 * x, 128) for x in range(4)]
        return out

    def gram():
        for k, h, a, n in blocks():
            sl = slice(32 * (k // 2), 32 * (k // 2) + 32)
            mm(ps(a, a + n), v("gle" if k % 2 == 0 else "glo", sl, slice(128 * h, 128 * h + 128)), v("gr", sl, slice(0, n)), False, False)

    def far_mm(h):
        for k in range(16):
            a = P6 + 128 * h + 8 * k
            mm(ps(a, a + 8), cmpcol("cmpf", h, k), v("blkf"))
        copy("s", v("fh", ALL, h, ALL), ps(P6 + 128 * h + 64, P6 + 128 * h + 128))

    def far_tree():
        for h in range(2):
            tt(v("m1", ALL, h, ALL), ps(P6 + 128 * h, P6 + 128 * h + 64), v("fh", ALL, h, ALL), A.max)
        tt(v("m2"), *halves("m1", 32), A.max)
        tt(v("m3"), *halves("m2", 16), A.max)

    def decide(t, lists):
        ts(v("ng"), v("wm"), 8.0, A.is_ge)
        for h in range(2):
            mm(ps(P7 + 128 * h, P7 + 128 * h + 128, 8), v("ng", ALL, h, ALL), v("idb"))
        copy("s", rows("ngt", 8, 0, NL), ps(P7, P7 + NL, 8))
        ts(v("go_"), v("wm"), 8.0, A.is_lt)
        tt(sub("ttl", 32, 40), v("wm"), v("ng"), A.mult)
        for q in range(3):
            tt(sub("sdg", 8 * q, 8 * q + 8), sub("sd", 8 * q, 8 * q + 8), v("go_"), A.mult)
        bl = blocks()
        for j, (k, h, a, n) in enumerate(bl):
            last = j == len(bl) - 1 or bl[j + 1][2] // 512 != a // 512
            mm(ps(a, a + n), rows("ngc", 8, 128 * k, 128 * k + 128), rows("ngt", 8, 0, n), False, last)
        for k, h, a, n in bl:
            r = v("rr", ALL, h, slice(k, k + 1))
            if a // 512 in (0, 2, 4):
                C("v", "tensor_reduce", out=r, in_=ps(a, a + n), axis=AxisListType.X, op=A.max)
            else:
                C("s", "activation", out=cols("junk", 0, n), in_=ps(a, a + n), func=AF.Relu, accum_out=r)
        ts(v("nd"), v("rr"), 0.5, A.is_lt)
        for q in range(3):
            tt(sub("ttl", 8 * q, 8 * q + 8), sub("sdg", 8 * q, 8 * q + 8), v("nd"), A.mult)
        tt(sub("ttl", 24, 32), v("go_"), v("nd"), A.mult)
        for h in range(2):
            mm(ps(P7 + 128 * h, P7 + 128 * h + 128, 40), v("ttl", ALL, h, ALL), v("idb"))
        copy("v", rows("t1", 40, 0, NL), ps(P7, P7 + NL, 40))
        mm(ps(P6, P6 + 16), v("idb"), v("li"), True, False)
        for i in range(16):
            mm(ps(P6, P6 + 16), rows("ew", 40, 15 - i, 143 - i), rows("t1", 40, i, NL, 16), False, i == 15)
        mm(row, rows("er2" if t == 2 else "er", 40, 0, 128), rows("t1", 40, 0, NL))
        ts(cols(lists, 0, 16), ps(P6, P6 + 16), float(DUMP + NL * t), A.add)

    def tell(src, width, land, sem):
        far = [c for c in T.cores if off_chip(topo, core, c)]
        near = [c for c in T.cores if c != core and not off_chip(topo, core, c)]
        tr = []
        for ds, en in ((far, far_engines(core, T, topo)), (near, near_engines(core, near[0], T, topo) if near else [])):
            if ds:
                tr.append((cols(src, 0, width), [(dst_id(topo, d), cols(land, width * rank, width * rank + width)) for d in ds], en, sem))
        fused(tr)

    told = sum(len(far_engines(c, T, topo)) if off_chip(topo, c, core) else len(near_engines(c, core, T, topo)) for c in T.cores if c != core)

    def gathered(name, land, width, t, sem):
        for k in range(NG):
            sl = slice(16 * k, 16 * k + 16)
            q = asked(rank, k, t)
            dma("y", sem, v(name, sl, ALL), v(land, sl, slice(width * q, width * q + width)))

    zrep("zrep", cols("z_s", 64, 320), "rep")
    dma("s", "d8", v("zql"), v("zqd"))
    dma("y", "d7", v("efq"), v("rl"))
    dma("s", "d5", cols("z_s", 320, NF), v("zf", ALL, slice(NL, 704)))
    dma("s", "d6", cols("z_s", 0, 64), v("zf", ALL, slice(704, NF)))
    dma("y", "d9", cols("eh_s", 320, NF), v("eh", ALL, slice(NL, 704)))
    dma("y", "d10", cols("eh_s", 0, 64), v("eh", ALL, slice(704, NF)))
    dma("y", "d11", cols("ef_s", 64, NF), v("ef", ALL, slice(0, 704)))
    dma("y", "d12", cols("ef_s", 0, 64), v("ef", ALL, slice(704, NF)))
    iota(v("ihi"), [[256, 3], [0, 256]], 0, 0)
    iota(v("ilo"), [[0, 3], [1, 256]], 0, 0)
    for q, i, c in ((0, 0, 2), (1, 1, 2), (2, 2, 2), (3, 3, -1), (4, 3, -1), (5, 3, -1), (6, 4, -1)):
        x = rows("err", 56, i, 128, 16)
        sel(x, x, [[1, 8]], A.not_equal, c, 8 * q, -1)
    for name, odd in (("ere", 0), ("ero", 1)):
        for q, i in ((0, 0), (1, 1), (2, 2), (6, 3), (3, 4), (4, 4), (5, 4)):
            x = rows(name, 56, 16 * odd + i, 128, 32)
            sel(x, x, [[2, 4]], A.not_equal, 1.0, 8 * q + odd, -1)
    sel(cols("mmk", 0, 512), v("ob"), [[0, 2], [-1, 256]], A.is_gt, -4096.0, 128, 1)
    sel(cols("mmk", 512, 1024), v("ob"), [[0, 4], [-1, 128]], A.is_gt, -4096.0, 0, 1)
    F["after"]("g", ["efq", "zql"])
    hp = helper_of(core, T, topo)
    he = topo.engines(core, hp)
    fused([(v("z_s"), [(dst_id(topo, hp), v("hz"))], he, "a_hz")])
    fused([(cols("tb", 0, NS), [(dst_id(topo, hp), v("hb"))], he, "a_hb")], "l_hb")

    for j in range(4):
        look(j, "cmph", "tb", NS, "offh", "zrep")
        if j == 1:
            key_mm(0)
    ts(v("ihi"), v("ihi"), cols("mk", 0, 1), A.mult)
    ts(v("ilo"), v("ilo"), cols("mk", 8, 9), A.mult)
    tt(v("ihl"), v("ihi"), v("ilo"), A.add)
    copy("v", v("offf"), v("efq"))
    key_mm(1)
    zrep("zrepf", v("zql"), "rep")
    for j in range(4):
        look(j, "cmpf", "tb", NS, "offf", "zrepf")
        if j == 0:
            home_tree(0)
        if j == 1:
            far_mm(0)
    far_mm(1)
    far_tree()
    for h in range(2):
        tt(v("wq", ALL, ALL, h), v("m3", ALL, h, slice(0, 8)), v("m3", ALL, h, slice(8, 16)), A.max)
    dst = [T.cores[asker(rank, k, 0)] for k in range(NG)]
    eng = singles(core, dst, T, topo)
    fused([(v("wq", ALL, k, ALL), [(dst_id(topo, dst[k]), v("wland", ALL, k, ALL))], [eng[k]], "a_wf") for k in range(NG)])
    arrive(v("wland"), "a_wf", NG)
    gram_rows()
    masks(range(6))
    gram()
    sel(rows("ngc", 8, 0, 1024), rows("zb", 8, 0, 1024), [[1, 8], [0, 128]], A.not_equal, -4096.0, 0, -1)
    for q, c in ((0, 256), (1, 16), (2, 1)):
        x = rows("ew", 40, 0, 143)
        sel(x, x, [[1, 143]], A.not_equal, c, -15 + 128 * q, -16)
    for name, q, c in (("er", 3, 128), ("er", 4, 1), ("er2", 4, 1)):
        x = rows(name, 40, 0, 128)
        sel(x, x, [[1, 8], [0, 16]], A.not_equal, c, 8 * q, -1)
    sel(v("onb"), cols("ob", 0, 128), [[-16, 8], [0, 16]], A.is_ge, 0.0, 0, 1)
    sel(v("onb"), v("onb"), [[16, 8], [0, 16]], A.is_ge, 0.0, 15, -1)
    sel(v("ntr"), v("ntr"), [[16, 8], [0, 16]], A.is_ge, 0.0, 15, -1)
    sel(v("ntr"), v("ntr"), [[-1, 128]], A.is_gt, 0.0, 0, 1)
    sel(v("ela"), cols("zb", 0, 144), [[1, 144]], A.not_equal, 1.0, -15, -1)
    sel(v("elb"), cols("zb", 0, 144), [[1, 144]], A.not_equal, 1.0, -14, -1)
    iota(cols("idf", 0, 64), [[1, 64]], 704, 0)
    iota(cols("idf", 64, NF), [[1, 704]], 0, 0)
    fill(v("occ"), -1.0)
    ts(v("ela"), v("ela"), cols("mk", 0, 1), A.mult)
    ts(v("elb"), v("elb"), cols("mk", 8, 9), A.mult)
    tt(v("el"), v("ela"), v("elb"), A.add)

    for h in range(2):
        tt(v("wm", ALL, h, ALL), v("whi", ALL, h, ALL), v("wland", ALL, ALL, h), A.max)
    decide(0, "w0")
    tell("w0", 16, "la0", "a_l0")
    arrive(v("la0"), "a_l0", told)
    for t in (1, 2):
        arrive(v("fd%d" % t), "a_f%d" % t, 2 * NG)
        arrive(v("zd%d" % t), "a_f%d" % t, 2 * NG)

    def scatter(table, lists, vals):
        copy("v", ind(v(table), cols(lists, 0, 16)), vals)

    def wrap(name):
        copy("v", cols(name, NS, DUMP), cols(name, 0, WR))

    def lanes(t, m0, m1):
        n = m1 - m0
        C("v", "scan", out=cols("scn", 0, n), data0=cols("ob", 0, n), data1=cols("uu", 0, n), initial=0.0, op0=A.mult, op1=A.add)
        mm(ps(0, n), v("ntr"), cols("uu", 0, n), True, False)
        mm(ps(0, n), v("onb"), cols("scn", 0, n), False, True)
        first = 0 if t == 1 else 704
        copy("v", cols("nrow", 0, 64), cols("ihl", first, first + 64))
        tt(cols("dst", 0, n), ps(0, n), cols("vb", 0, n), A.max)
        ts(cols("dsu", 0, n), cols("dst", 0, n), 63.0, A.add)
        copy("v", ind(cols("nrow", 0, 2048), cols("dsu", 0, n)), cols("ihl", 16 * m0, 16 * m1))

    def lanes_end(lists):
        for i in range(16):
            mm(ps(512, 528), cols("el", 15 - i, 143 - i), cols("nrow", i, NL, 16), i == 0, i == 15)
        copy("v", cols(lists, 16, 32), ps(512, 528))

    def step(t):
        L, tabf, lnf = "w%d" % t, "f%d" % t, "lnf%d" % t
        ln = cols(L, 16, 32)
        copy("v", v("zl"), ind(v("z_s"), ln))
        C("s", "activation", out=v("dc"), in_=ind(v("st"), ln), func=AF.Identity, bias=ckc)
        tt(v("xp"), ind(v("eh_s"), ln), v("dc"), A.add)
        ts(v("offh"), v("xp"), ckc, A.subtract)
        zrep("zrep", v("zl"), "rep")
        copy("s", v("dl"), ind(v("st"), ln))
        copy("s", v(lnf), ind(v("idf"), ln))
        if t == 2:
            for a, b in ((P6, 0), (P7, 384)):
                mm(ps(a, a + 384), v("idb"), cols("st", b, b + 384), True, False)
                mm(ps(a, a + 384), v("idb"), cols("ydm", b, b + 384), False, True)
                copy("s", cols("stc", b, b + 384), ps(a, a + 384))
            copy("s", v("st1c"), ind(v("stc"), cols("w1", 16, 32)))
        masks((2, 3, 4, 5))
        for j in range(4):
            look(j, "cmph", "tb", DUMP, "offh", "zrep")
            if j == 1:
                key_mm(0)
                tt(v("xf"), ind(v("ef_s"), ln), v("dc"), A.add)
            if j == 2:
                ts(v("offf"), v("xf"), ckc, A.subtract)
        key_mm(1)
        if t == 1:
            scatter("f1", "u10", cols("zf1", 64, 320))
        else:
            scatter("f2", "u21", v("zu"))
        wrap(tabf)
        home_tree(t)
        gram_rows()
        masks((0, 1))
        for j in range(4):
            look(j, "cmpf", tabf, DUMP, "offf", "zrep")
            if j == 1:
                far_mm(0)
                gram()
        far_mm(1)
        far_tree()
        tt(v("m4"), *halves("m3", 8), A.max)
        tt(v("wm"), v("whi"), v("m4"), A.max)
        decide(t, L)

    ts(cols("uu", 0, 16), ps(P6, P6 + 16), -0.5, A.is_ge)
    ts(cols("dst", 0, 16), ps(P6, P6 + 16), -0.5, A.is_lt)
    tt(cols("vb", 0, 16), cols("dst", 0, 16), cols("yc", 4, 20), A.mult)
    dma("y", "d13", cols("f1", 0, NS), v("fd1"))
    dma("y", "d14", v("zf1"), v("zd1"))
    gathered("u10", "la0", 16, 1, "d15")
    gathered("u20", "la0", 16, 2, "d16")
    dma("y", "d17", cols("f2", 0, NS), v("fd2"))
    dma("y", "d18", v("zf2"), v("zd2"))
    lanes(1, 4, 32)
    copy("v", cols("st", 64, 320), row)
    scatter("tb", "w0", cols("z_s", 64, 320))
    wrap("tb")
    lanes_end("w1")
    scatter("occ", "w0", cols("idf", 64, 320))
    step(1)
    tell("w1", 32, "la1", "a_l1")
    arrive(v("la1"), "a_l1", told)
    gathered("u21", "la1", 32, 2, "d19")
    scatter("occ", "w1", v("lnf1"))
    tt(v("st1"), v("dl"), row, A.add)
    copy("v", ind(v("st"), cols("w1", 16, 32)), v("st1"))
    tt(v("b1"), ind(v("occ"), v("w0")), cols("idf", 64, 320), A.not_equal)
    ts(v("zu"), v("b1"), -127.0, A.mult)
    tt(cols("st", 64, 320), cols("st", 64, 320), v("zu"), A.add)
    for i in range(16):
        mm(ps(640, 672), cols("el", 15 - i, 143 - i), cols("st", i, 512, 16), i == 0, i == 15)
    scatter("tb", "w1", v("zl"))
    wrap("tb")
    ts(cols("uu", 0, 32), ps(640, 672), 255.0, A.is_lt)
    ts(cols("dst", 0, 32), ps(640, 672), 255.0, A.is_ge)
    fill(cols("vb", 32, 48), 0.0)
    fill(cols("uu", 32, 48), 1.0)
    tt(cols("vb", 0, 32), cols("dst", 0, 32), cols("yc", 0, 32), A.mult)
    lanes(2, 0, 44)
    ts(v("ydm"), v("st"), 128.0, A.is_ge, -128.0, A.mult)
    lanes_end("w2")
    scatter("f2", "u20", cols("zf2", 64, 320))
    copy("s", v("zu"), ind(v("zf2"), cols("u21", 16, 32)))
    step(2)
    scatter("tb", "w2", v("zl"))
    dma("y", "d20", v("yt"), cols("tb", 0, NS))
    scatter("occ", "w2", v("lnf2"))
    dma("s", "d21", v("yo"), v("occ", slice(0, 128, 16), slice(0, NS)))
    tt(v("st2"), v("dl"), row, A.add)
    tt(v("zu"), ind(v("occ"), cols("w1", 0, 16)), v("lnf1"), A.not_equal)
    tt(v("st1c"), v("st1c"), v("zu"), A.add)
    copy("v", ind(v("stc"), cols("w1", 16, 32)), v("st1c"))
    tt(v("b3"), ind(v("occ"), v("w0")), cols("idf", 64, 320), A.not_equal)
    tt(v("b3"), v("b3"), v("b1"), A.is_gt)
    copy("v", ind(v("stc"), cols("w2", 16, 32)), v("st2"))
    tt(cols("stc", 64, 320), cols("stc", 64, 320), v("b3"), A.add)
    dma("y", "d22", v("yd", ALL, slice(0, 704)), v("stc", slice(0, 128, 16), slice(64, NF)))
    dma("s", "d23", v("yd", ALL, slice(704, NF)), v("stc", slice(0, 128, 16), slice(0, 64)))
    F["finish"]()


def rank_program(g, core, T, topo):
    rank = T.rank_of(core)
    if rank is not None:
        rank_main(g, core, rank, T, topo)
        return
    for c in topo.cores_of(core):
        if T.rank_of(c) is not None and helper_of(c, T, topo) == core:
            helper_main(g, core, T.rank_of(c), T, topo)
            return
